import numpy as np
import ml_dtypes


def mxq(x, axis, fmt="e4m3"):
    dtype, down = {"e4m3": (ml_dtypes.float8_e4m3fn, 7), "e5m2": (ml_dtypes.float8_e5m2, 14)}[fmt]
    v = np.moveaxis(np.asarray(x, np.float32).astype(ml_dtypes.bfloat16).astype(np.float64), axis, -1)
    blocks = v.reshape(v.shape[:-1] + (-1, 32))
    amax = np.abs(blocks).max(-1, keepdims=True)
    byte = np.maximum(np.where(amax > 0, np.frexp(amax)[1] - 1 + 127, 0) - down, 1)
    scale = np.exp2(byte - 127.0)
    codes = (blocks / scale).astype(np.float32).astype(dtype).astype(np.float64)
    return np.moveaxis((codes * scale).reshape(v.shape), -1, axis)


WIDE = False


def mx_kscale(k):
    if not WIDE:
        return np.ones(k)
    levels = np.array([10, -10, 5, -5, 0])
    if k % 512:
        return np.exp2(np.random.permutation(np.resize(levels, k // 32))).repeat(32)
    a = np.empty((k // 512, 16))
    for p in range(k // 512):
        a[p, :8] = np.random.permutation(np.resize(levels, 8))
        for g in range(8):
            far = levels[np.abs(levels - a[p, g]) >= 10]
            a[p, g + 8] = far[np.random.randint(len(far))]
    return np.exp2(a.ravel()).repeat(32)


def f64(x):
    return np.asarray(x).astype(np.float64)


def striped(idx):
    return np.tile(idx.reshape(-1, 16).T, (8, 1)).astype(np.uint16)


def unstriped(offs):
    return offs[:16].T.reshape(-1).astype(np.int64)


E2M1 = np.array([0.0, 0.5, 1.0, 1.5, 2.0, 3.0, 4.0, 6.0, -0.0, -0.5, -1.0, -1.5, -2.0, -3.0, -4.0, -6.0])


def pack_weight(w, fmt):
    k, n = w.shape
    w = f64(np.asarray(w, np.float32).astype(ml_dtypes.bfloat16)).reshape(k // 32, 32, n)
    amax = np.abs(w).max(1)
    if fmt == "e4m3":
        byte = np.frexp(amax)[1] - 1 + 127 - 7
    else:
        mant, ex = np.frexp(amax / 6.0)
        byte = np.where(mant > 0.5, ex, ex - 1) + 127
    byte = np.clip(np.where(amax > 0, byte, 1), 1, 254)
    scaled = (w * np.exp2(127.0 - byte)[:, None, :]).reshape(k, n).astype(np.float32)
    by_word = np.ascontiguousarray(scaled.reshape(k // 512, 128, 4, n).transpose(0, 1, 3, 2))
    if fmt == "e4m3":
        words = by_word.astype(ml_dtypes.float8_e4m3fn).view(np.uint8)
    else:
        c = by_word.astype(ml_dtypes.float4_e2m1fn).view(np.uint8) & 0xF
        words = (c[..., 0::2] | (c[..., 1::2] << 4)).reshape(k // 512, 128, 2 * n)
    return np.ascontiguousarray(words), np.ascontiguousarray(byte.astype(np.uint8).reshape(k // 512, 16, n))


def unpack_weight(words, scales, fmt):
    g, _, n = scales.shape
    words = np.ascontiguousarray(words).reshape(g, 128, n, -1)
    if fmt == "e4m3":
        vals = words.view(ml_dtypes.float8_e4m3fn).astype(np.float64)
    else:
        nib = np.empty((g, 128, n, 4), np.uint8)
        nib[..., 0::2] = words & 0xF
        nib[..., 1::2] = words >> 4
        vals = E2M1[nib]
    vals = vals * np.repeat(np.exp2(scales.astype(np.float64) - 127.0), 8, axis=1)[..., None]
    return vals.transpose(0, 1, 3, 2).reshape(g * 512, n)


def gelu(v):
    return 0.5 * v * (1.0 + np.tanh(np.sqrt(2.0 / np.pi) * (v + 0.044715 * v**3)))


def often(T, S):
    return np.random.permutation(T)[(T * np.random.uniform(0, 1, S) ** 4).astype(np.int64)]


K, K2, H, N, T, S, P = 1024, 512, 1024, 512, 4096, 1024, 512

def setup_inputs():
    n = np.random.standard_normal
    s, s2, u = mx_kscale(K)[:, None], mx_kscale(K2)[:, None], mx_kscale(H)[:, None]
    d = {}
    d["tab_words"], d["tab_scales"] = pack_weight(n((K, T)) * s, "e4m3")
    d["tab2_words"], d["tab2_scales"] = pack_weight(n((K2, T)) * s2, "e4m3")
    d["tab3_words"], d["tab3_scales"] = pack_weight(n((K2, T)) * s2, "e4m3")
    d["offs"] = striped(np.random.permutation(T)[:S])
    d["offs2"] = striped(np.random.permutation(T)[:S])
    d["offs3"] = striped(np.random.permutation(T)[:S])
    d["pos1"] = striped(np.random.permutation(S)[:P])
    d["pos2"] = striped(often(S, P))
    d["pos3"] = striped(often(S, P))
    d["w1"] = (n((K, H)) / K ** 0.5 / s * u.T).astype(np.float32)
    d["w2_words"], d["w2_scales"] = pack_weight(n((K2, H)) / K2 ** 0.5 / s2 * u.T, "e4m3")
    d["w3"] = (n((K2, H)) / K2 ** 0.5 / s2 * u.T).astype(np.float32)
    d["w4_words"], d["w4_scales"] = pack_weight(1.2 * n((H, N)) / H ** 0.5 / u, "e2m1")
    d["bias"] = (0.6 * n(N)).astype(np.float32)
    d["w5"] = (0.6 * n((H, N)) / H ** 0.5 / u).astype(np.float32)
    return d

def reference(tab_words, tab_scales, tab2_words, tab2_scales, tab3_words, tab3_scales, offs, offs2, offs3,
              pos1, pos2, pos3, w1, w2_words, w2_scales, w3, w4_words, w4_scales, bias, w5):
    v = unpack_weight(tab_words, tab_scales, "e4m3")[:, unstriped(offs)]
    v2 = unpack_weight(tab2_words, tab2_scales, "e4m3")[:, unstriped(offs2)]
    v3 = unpack_weight(tab3_words, tab3_scales, "e4m3")[:, unstriped(offs3)]
    a = mxq(f64(w1), 0, "e4m3").T @ v
    b = unpack_weight(w2_words, w2_scales, "e4m3").T @ v2
    d = mxq(f64(w3), 0, "e4m3").T @ v3
    course = b[:, unstriped(pos2)]
    top = np.maximum(a[:, unstriped(pos1)], course)
    low = np.minimum(course, d[:, unstriped(pos3)])
    z = mxq(top - low, 0, "e4m3")
    y = (unpack_weight(w4_words, w4_scales, "e2m1").T @ z) + f64(bias)[:, None]
    bent = y / (1.0 + np.exp(-y))
    return bent + (mxq(f64(w5), 0, "e4m3").T @ z)

@@ -1,0 +1,282 @@
+from contextlib import ExitStack
+
+import concourse.mybir as mybir
+
+F32 = mybir.dt.float32
+BF16 = mybir.dt.bfloat16
+I32 = mybir.dt.int32
+U32 = mybir.dt.uint32
+U16 = mybir.dt.uint16
+U8 = mybir.dt.uint8
+FP8X4 = mybir.dt.float8_e4m3fn_x4
+FP4X4 = mybir.dt.float4_e2m1fn_x4
+ALU = mybir.AluOpType
+ACT = mybir.ActivationFunctionType
+
+K, K2, H, N, T, S, J = 1024, 512, 1024, 512, 4096, 1024, 512
+P = 128
+PACK = 4
+KP = P * PACK
+BANK = 512
+CHUNKS = ((0, 256), (256, 384), (384, 512))
+D_TAGS = ("S0", "S1", "S2", "S8", "S9", "S10", "S11", "S7")
+A_TAGS = ("S0", "S2", "S5", "S9", "S3", "S4", "S10", "S0")
+FLOPS = 2 * (K + 2 * K2) * H * S + 2 * 2 * H * N * J
+
+
+def tile_list_handicap_weight_book_kernel(
+    tc, tab_words, tab_scales, tab2_words, tab2_scales, tab3_words, tab3_scales, offs, offs2, offs3,
+    pos1, pos2, pos3, w1, w2_words, w2_scales, w3, w4_words, w4_scales, bias, w5, out,
+):
+    nc = tc.nc
+    with ExitStack() as ctx:
+        lists = ctx.enter_context(tc.tile_pool(name="lists", bufs=1))
+        keep = ctx.enter_context(tc.tile_pool(name="keep", bufs=1))
+        ring = ctx.enter_context(tc.tile_pool(name="ring", bufs=2))
+        psum = ctx.enter_context(tc.psum_pool(name="psum", bufs=8))
+
+        def load_list(src, name):
+            t = lists.tile(list(src.shape), U16, name=name)
+            nc.sync.dma_start(t[:], src)
+            return t
+
+        def zeroed_plane(width, name):
+            t = keep.tile([P, width], U8, name=name, align_bytes=64)
+            nc.vector.memset(t[:].bitcast(I32), 0)
+            return t
+
+        def load_plane(queue, t, scales, first):
+            passes = scales.shape[0]
+            for q in range(4):
+                lo = 32 * q + first
+                queue.dma_start(t[lo:lo + 4 * passes, :].bitcast(I32), scales[:, 4 * q:4 * q + 4, :].bitcast(I32))
+
+        def load_words(words, name, width, tag):
+            t = keep.tile([P, width], U32, name=name, tag=tag, align_bytes=64)
+            nc.sync.dma_start(t[:].bitcast(I32), words.rearrange("p t i -> p (t i)").bitcast(I32))
+            return t
+
+        def load_raw(src, tag):
+            t = keep.tile([P, PACK, H], F32, name="raw", tag=tag, align_bytes=64)
+            nc.sync.dma_start(t[:], src.rearrange("(p j) c -> p j c", j=PACK))
+            return t
+
+        def gather(window, offsets, dtype, name, tag):
+            t = keep.tile([P, S], dtype, name=name, tag=tag, align_bytes=64)
+            nc.vector.tensor_copy(t[:], window[:].indirect(offsets[:]))
+            return t
+
+        def quantize(pieces, name, tag):
+            codes = keep.tile([P, H], U32, name=name + "_codes", tag=tag, align_bytes=64)
+            scales = keep.tile([P, H], U8, name=name + "_scales", align_bytes=64)
+            width = H // len(pieces)
+            for i, grouped in enumerate(pieces):
+                cols = slice(width * i, width * (i + 1))
+                nc.vector.quantize_mx(out=codes[:, cols].bitcast(FP8X4), scales=scales[:, cols], in_=grouped[:])
+            return codes, scales
+
+        def cast_gpsimd(raw):
+            grouped = ring.tile([P, PACK * H], BF16, name="grouped", tag="grouped", align_bytes=64)
+            dst = grouped[:].rearrange("p (b t m j) -> p b m t j", b=2, t=4, j=PACK)
+            src = raw[:].rearrange("p j (b m t) -> p b m t j", b=2, t=4)
+            for b in range(2):
+                nc.gpsimd.tensor_scalar(dst[:, b], src[:, b], 1.0, 0.0, ALU.mult, ALU.add)
+            return grouped
+
+        def cast_scalar(raw, tags):
+            src = raw[:].rearrange("p (u e) (b m t) -> p b m u t e", u=2, b=2, t=4)
+            pieces = []
+            for b in range(2):
+                grouped = keep.tile([P, PACK * KP], BF16, name="grouped", tag=tags[b], align_bytes=64)
+                nc.scalar.copy(grouped[:].rearrange("p (t m u e) -> p m u t e", t=4, u=2, e=2), src[:, b])
+                pieces.append(grouped)
+            return pieces
+
+        def interleave(copy, dst, src):
+            copy(dst.rearrange("p (c i j) -> p c j i", i=4, j=PACK), src.rearrange("p j (c i) -> p c j i", i=4))
+
+        def first_stage(r, passes, tag):
+            window = keep.tile([P, S], F32, name="window", tag=tag, align_bytes=64)
+            cols = slice(P * r, P * (r + 1))
+            for h in range(S // BANK):
+                acc = psum.tile([P, BANK], F32, name="acc", tag="acc")
+                half = slice(BANK * h, BANK * (h + 1))
+                for a, (wc, ws, vc, vs, first) in enumerate(passes):
+                    nc.tensor.matmul_mx(out=acc[:], lhsT=wc[:, cols].bitcast(FP8X4), lhsT_scale=ws[:, cols],
+                                        rhs=vc[:, half].bitcast(FP8X4), rhs_scale=vs[first:, half],
+                                        start=(a == 0), stop=(a == len(passes) - 1))
+                nc.scalar.copy(window[:, half], acc[:])
+            return window
+
+        ts2 = zeroed_plane(T, "ts2")
+        w2s_raw = zeroed_plane(H, "w2s_raw")
+        ts3 = zeroed_plane(T, "ts3")
+        ts1 = zeroed_plane(T, "ts1")
+        w4s = zeroed_plane(2 * N, "w4s")
+        o2 = load_list(offs2, "o2")
+        w2_raw = load_words(w2_words[0], "w2_raw", H, "w2_raw")
+        load_plane(nc.sync, ts2, tab2_scales, 4)
+        load_plane(nc.sync, w2s_raw, w2_scales, 0)
+        o3 = load_list(offs3, "o3")
+        load_plane(nc.sync, ts3, tab3_scales, 0)
+        tw2 = load_words(tab2_words[0], "tw2", T, "T2")
+        o1 = load_list(offs, "o1")
+        load_plane(nc.sync, ts1, tab_scales, 8)
+        raw3 = load_raw(w3, "A")
+        p2 = load_list(pos2, "p2")
+        tw3 = load_words(tab3_words[0], "tw3", T, "T3")
+        p3 = load_list(pos3, "p3")
+        raw1a = load_raw(w1[0:KP, :], "B")
+
+        vs2 = gather(ts2, o2, U8, "vs2", "vs2")
+        w2s = keep.tile([P, H], U8, name="w2s", align_bytes=64)
+        nc.vector.tensor_copy(w2s[:].rearrange("p (b t m) -> p b t m", b=2, t=4),
+                              w2s_raw[:].rearrange("p (b m t) -> p b t m", b=2, t=4))
+        w2c = keep.tile([P, H], U32, name="w2c", align_bytes=64)
+        nc.scalar.copy(w2c[:].rearrange("p (b t m) -> p b m t", b=2, t=4),
+                       w2_raw[:].rearrange("p (b m t) -> p b m t", b=2, t=4))
+        vs3 = gather(ts3, o3, U8, "vs3", "vs3")
+        vc2 = gather(tw2, o2, U32, "vc2", "vc2")
+        vs1 = gather(ts1, o1, U8, "vs1", "vs1")
+        g3 = cast_gpsimd(raw3)
+        raw1b = load_raw(w1[KP:2 * KP, :], "C")
+        p1 = load_list(pos1, "p1")
+        tw0 = load_words(tab_words[0], "tw0", T, "T2")
+        course = keep.tile([P, 8, J], F32, name="course")
+        for r in range(8):
+            window = first_stage(r, [(w2c, w2s, vc2, vs2, 4)], "S%d" % r)
+            nc.vector.tensor_copy(course[:, r, :], window[:].indirect(p2[:]))
+            if r == 3:
+                vc3 = gather(tw3, o3, U32, "vc3", "S3")
+                tw1 = load_words(tab_words[1], "tw1", T, "T3")
+            if r == 4:
+                w3c, w3s = quantize([g3], "w3", "S4")
+
+        g1a = cast_gpsimd(raw1a)
+        w4c = keep.tile([P, 2 * 2 * N], U8, name="w4c", align_bytes=64)
+        nc.sync.dma_start(w4c[:].bitcast(I32).rearrange("p (a c) -> p a c", a=2),
+                          w4_words.bitcast(I32).rearrange("a p c -> p a c"))
+        for q in range(4):
+            nc.sync.dma_start(w4s[32 * q:32 * q + 4, :].bitcast(I32).rearrange("p (a c) -> p a c", a=2),
+                              w4_scales[:, 4 * q:4 * q + 4, :].bitcast(I32).rearrange("a r c -> r a c"))
+        bias_t = keep.tile([P, N // P], F32, name="bias_t")
+        with nc.allow_non_contiguous_dma(reason="one bias value a partition"):
+            nc.sync.dma_start(bias_t[:], bias.rearrange("(c p) -> p c", p=P))
+
+        below = []
+        for b in range(2):
+            if b == 1:
+                vc0 = gather(tw0, o1, U32, "vc0", "S8")
+                g1b = cast_scalar(raw1b, ("S5", "S6"))
+                w1bc, w1bs = quantize(g1b, "w1b", "w1bc")
+                vc1 = gather(tw1, o1, U32, "vc1", "S6")
+                raw5 = keep.tile([P, 2, PACK, N], F32, name="raw", tag="C", align_bytes=64)
+                for a in range(2):
+                    nc.sync.dma_start(raw5[:, a], w5[KP * a:KP * (a + 1), :].rearrange("(p j) c -> p j c", j=PACK))
+            z = keep.tile([P, PACK, J], F32, name="z", tag=("A", "T3")[b], align_bytes=64)
+            below.append(z)
+            for t in range(PACK):
+                r = PACK * b + t
+                window = first_stage(r, [(w3c, w3s, vc3, vs3, 0)], D_TAGS[r])
+                nc.vector.tensor_tensor(z[:, t, :], window[:].indirect(p3[:]), course[:, r, :], ALU.subtract)
+                if r == 1:
+                    w1ac, w1as = quantize([g1a], "w1a", "S1")
+
+        a_passes = [(w1ac, w1as, vc0, vs1, 8), (w1bc, w1bs, vc1, vs1, 12)]
+        zq = []
+        for b in range(2):
+            zq.append((keep.tile([P, J], U32, name="z_codes%d" % b, align_bytes=64),
+                       keep.tile([P, J], U8, name="z_scales%d" % b, align_bytes=64)))
+
+        def join(b, windows, c0, c1, lead):
+            for t in range(PACK):
+                nc.vector.tensor_tensor(lead[:, t, :], windows[t][:].indirect(p1[:, c0 // 16:c1 // 16]),
+                                        course[:, PACK * b + t, c0:c1], ALU.subtract)
+            z = spread[b][:, :, c0:c1]
+            nc.vector.scalar_tensor_tensor(z, lead[:], 0.0, z, ALU.max, ALU.add)
+
+        def round_z(b, c0, c1, tag):
+            rounded = keep.tile([P, PACK * (c1 - c0)], BF16, name="rounded", tag=tag, align_bytes=64)
+            interleave(nc.scalar.copy, rounded[:], spread[b][:, :, c0:c1])
+            return rounded
+
+        def quantize_z(b, c0, c1, rounded):
+            nc.vector.quantize_mx(out=zq[b][0][:, c0:c1].bitcast(FP8X4), scales=zq[b][1][:, c0:c1], in_=rounded[:])
+
+        def lead_tile(pool, ci, tag):
+            c0, c1 = CHUNKS[ci]
+            return pool.tile([P, PACK, c1 - c0], F32, name="lead", tag=tag, align_bytes=64)
+
+        def rectify(b, tag):
+            s = keep.tile([P, PACK, J], F32, name="spread", tag=tag, align_bytes=64)
+            nc.scalar.activation(s[:], below[b][:], ACT.Relu, scale=-1.0)
+            return s
+
+        spread = [rectify(0, "B")]
+        windows0 = [first_stage(t, a_passes, A_TAGS[t]) for t in range(PACK)]
+        join(0, windows0, 0, J, keep.tile([P, PACK, J], F32, name="lead", tag="L", align_bytes=64))
+        windows1 = [first_stage(PACK + t, a_passes, A_TAGS[PACK + t]) for t in range(PACK)]
+        rounded0 = round_z(0, 0, J, "zb0")
+        spread.append(rectify(1, "L"))
+        g5 = [keep.tile([P, PACK * N], BF16, name="g5", tag=tag, align_bytes=64) for tag in ("S11", "S7")]
+        for a in range(2):
+            interleave(nc.vector.tensor_copy, g5[a][:], raw5[:, a])
+        w5c, w5s = quantize(g5, "w5", "w5c")
+
+        tiles_n = N // P
+        banks = []
+        for c0, c1 in CHUNKS:
+            per_bank = BANK // (c1 - c0)
+            banks.append([[psum.tile([P, BANK], F32, name="acc", tag="acc") for n0 in range(0, tiles_n, per_bank)]
+                          for which in range(2)])
+        tail = keep.tile([P, 2, tiles_n * J], F32, name="tail", tag="T2", align_bytes=64)
+
+        def second_stage(ci, which, b):
+            c0, c1 = CHUNKS[ci]
+            width = c1 - c0
+            per_bank = BANK // width
+            for n in range(tiles_n):
+                col = N * b + P * n
+                if which == 0:
+                    lhsT, lhsT_scale = w4c[:, 2 * col:2 * (col + P)].bitcast(FP4X4), w4s[:, col:col + P]
+                else:
+                    lhsT, lhsT_scale = w5c[:, col:col + P].bitcast(FP8X4), w5s[:, col:col + P]
+                slot = n % per_bank
+                nc.tensor.matmul_mx(out=banks[ci][which][n // per_bank][:, width * slot:width * (slot + 1)],
+                                    lhsT=lhsT, lhsT_scale=lhsT_scale,
+                                    rhs=zq[b][0][:, c0:c1].bitcast(FP8X4), rhs_scale=zq[b][1][:, c0:c1],
+                                    start=(b == 0 and slot == 0), stop=(b == 1 and slot == per_bank - 1))
+
+        def finish(ci):
+            c0, c1 = CHUNKS[ci]
+            width = c1 - c0
+            per_bank = BANK // width
+            base = tiles_n * c0
+            for n in range(tiles_n):
+                slot = n % per_bank
+                nc.scalar.activation(tail[:, 0, base + width * n:base + width * (n + 1)],
+                                     banks[ci][0][n // per_bank][:, width * slot:width * (slot + 1)],
+                                     ACT.Silu, bias=bias_t[:, n:n + 1])
+            for i, bank in enumerate(banks[ci][1]):
+                cols = slice(base + BANK * i, base + BANK * (i + 1))
+                nc.vector.tensor_tensor(tail[:, 1, cols], bank[:], tail[:, 0, cols], ALU.add)
+                nc.sync.dma_start(
+                    out.rearrange("(n p) j -> p n j", p=P)[:, per_bank * i:per_bank * (i + 1), c0:c1],
+                    tail[:, 1, cols].rearrange("p (n j) -> p n j", j=width))
+
+        join(1, windows1, *CHUNKS[0], lead_tile(keep, 0, "C"))
+        rounded = round_z(1, *CHUNKS[0], "zb1")
+        quantize_z(0, 0, J, rounded0)
+        for which in range(2):
+            for ci in range(len(CHUNKS)):
+                second_stage(ci, which, 0)
+        join(1, windows1, *CHUNKS[1], lead_tile(keep, 1, "zb0"))
+        for ci in range(len(CHUNKS)):
+            quantize_z(1, *CHUNKS[ci], rounded)
+            second_stage(ci, 0, 1)
+            second_stage(ci, 1, 1)
+            if ci + 1 < len(CHUNKS):
+                rounded = round_z(1, *CHUNKS[ci + 1], "zb%d" % (ci + 2))
+            if ci + 2 < len(CHUNKS):
+                join(1, windows1, *CHUNKS[ci + 2], lead_tile(keep, ci + 2, "zb1"))
+            finish(ci)

@@ -19,8 +19,10 @@ PACK = 4
 KP = P * PACK
 BANK = 512
 CHUNKS = ((0, 256), (256, 384), (384, 512))
-D_TAGS = ("S0", "S1", "S2", "S8", "S9", "S10", "S11", "S7")
-A_TAGS = ("S0", "S2", "S5", "S9", "S3", "S4", "S10", "S0")
+JOINS = ((0, 384), (384, 512))
+EARLY = 6
+D_TAGS = ("S0", "S13", "S2", "S8", 0, 1, 2, 3)
+A_TAGS = ("S6", "S7", "S4", "S5", "S3", "S0", 0, 1)
 FLOPS = 2 * (K + 2 * K2) * H * S + 2 * 2 * H * N * J
 
 
@@ -32,7 +34,7 @@ def tile_list_handicap_weight_book_kernel(
     with ExitStack() as ctx:
         lists = ctx.enter_context(tc.tile_pool(name="lists", bufs=1))
         keep = ctx.enter_context(tc.tile_pool(name="keep", bufs=1))
-        ring = ctx.enter_context(tc.tile_pool(name="ring", bufs=2))
+        placed = ctx.enter_context(tc.tile_pool(name="placed", bufs=1))
         psum = ctx.enter_context(tc.psum_pool(name="psum", bufs=8))
 
         def load_list(src, name):
@@ -50,6 +52,14 @@ def tile_list_handicap_weight_book_kernel(
             for q in range(4):
                 lo = 32 * q + first
                 queue.dma_start(t[lo:lo + 4 * passes, :].bitcast(I32), scales[:, 4 * q:4 * q + 4, :].bitcast(I32))
+
+        def filled_plane(scales, name):
+            width = scales.shape[2]
+            t = keep.tile([P, width], U8, name=name, align_bytes=64)
+            for q in range(4):
+                live = scales[:, 4 * q:4 * q + 4, :].bitcast(I32)
+                nc.sync.dma_start(t[32 * q:32 * (q + 1), :].bitcast(I32), live.broadcast_to([8, 4, width // 4]))
+            return t
 
         def load_words(words, name, width, tag):
             t = keep.tile([P, width], U32, name=name, tag=tag, align_bytes=64)
@@ -75,28 +85,20 @@ def tile_list_handicap_weight_book_kernel(
                 nc.vector.quantize_mx(out=codes[:, cols].bitcast(FP8X4), scales=scales[:, cols], in_=grouped[:])
             return codes, scales
 
-        def cast_gpsimd(raw):
-            grouped = ring.tile([P, PACK * H], BF16, name="grouped", tag="grouped", align_bytes=64)
-            dst = grouped[:].rearrange("p (b t m j) -> p b m t j", b=2, t=4, j=PACK)
-            src = raw[:].rearrange("p j (b m t) -> p b m t j", b=2, t=4)
-            for b in range(2):
-                nc.gpsimd.tensor_scalar(dst[:, b], src[:, b], 1.0, 0.0, ALU.mult, ALU.add)
-            return grouped
-
-        def cast_scalar(raw, tags):
+        def cast_scalar(raw, b, tag):
             src = raw[:].rearrange("p (u e) (b m t) -> p b m u t e", u=2, b=2, t=4)
-            pieces = []
-            for b in range(2):
-                grouped = keep.tile([P, PACK * KP], BF16, name="grouped", tag=tags[b], align_bytes=64)
-                nc.scalar.copy(grouped[:].rearrange("p (t m u e) -> p m u t e", t=4, u=2, e=2), src[:, b])
-                pieces.append(grouped)
-            return pieces
+            grouped = keep.tile([P, PACK * KP], BF16, name="grouped", tag=tag, align_bytes=64)
+            nc.scalar.copy(grouped[:].rearrange("p (t m u e) -> p m u t e", t=4, u=2, e=2), src[:, b])
+            return grouped
 
         def interleave(copy, dst, src):
             copy(dst.rearrange("p (c i j) -> p c j i", i=4, j=PACK), src.rearrange("p j (c i) -> p c j i", i=4))
 
         def first_stage(r, passes, tag):
-            window = keep.tile([P, S], F32, name="window", tag=tag, align_bytes=64)
+            if isinstance(tag, int):
+                window = placed.tile([P, S], F32, name="window%d_%d" % (len(passes), r), offset=4 * S * tag, align_bytes=64)
+            else:
+                window = keep.tile([P, S], F32, name="window", tag=tag, align_bytes=64)
             cols = slice(P * r, P * (r + 1))
             for h in range(S // BANK):
                 acc = psum.tile([P, BANK], F32, name="acc", tag="acc")
@@ -108,18 +110,16 @@ def tile_list_handicap_weight_book_kernel(
                 nc.scalar.copy(window[:, half], acc[:])
             return window
 
-        ts2 = zeroed_plane(T, "ts2")
-        w2s_raw = zeroed_plane(H, "w2s_raw")
         ts3 = zeroed_plane(T, "ts3")
         ts1 = zeroed_plane(T, "ts1")
         w4s = zeroed_plane(2 * N, "w4s")
         o2 = load_list(offs2, "o2")
-        w2_raw = load_words(w2_words[0], "w2_raw", H, "w2_raw")
-        load_plane(nc.sync, ts2, tab2_scales, 4)
-        load_plane(nc.sync, w2s_raw, w2_scales, 0)
-        o3 = load_list(offs3, "o3")
-        load_plane(nc.sync, ts3, tab3_scales, 0)
+        ts2 = filled_plane(tab2_scales, "ts2")
+        w2s_raw = filled_plane(w2_scales, "w2s_raw")
         tw2 = load_words(tab2_words[0], "tw2", T, "T2")
+        w2_raw = load_words(w2_words[0], "w2_raw", H, "w2_raw")
+        o3 = load_list(offs3, "o3")
+        load_plane(nc.sync, ts3, tab3_scales, 4)
         o1 = load_list(offs, "o1")
         load_plane(nc.sync, ts1, tab_scales, 8)
         raw3 = load_raw(w3, "A")
@@ -127,6 +127,9 @@ def tile_list_handicap_weight_book_kernel(
         tw3 = load_words(tab3_words[0], "tw3", T, "T3")
         p3 = load_list(pos3, "p3")
         raw1a = load_raw(w1[0:KP, :], "B")
+        raw1b = placed.tile([P, PACK, H], F32, name="raw1b", offset=0, align_bytes=64)
+        nc.sync.dma_start(raw1b[:], w1[KP:2 * KP, :].rearrange("(p j) c -> p j c", j=PACK))
+        p1 = load_list(pos1, "p1")
 
         vs2 = gather(ts2, o2, U8, "vs2", "vs2")
         w2s = keep.tile([P, H], U8, name="w2s", align_bytes=64)
@@ -135,24 +138,29 @@ def tile_list_handicap_weight_book_kernel(
         w2c = keep.tile([P, H], U32, name="w2c", align_bytes=64)
         nc.scalar.copy(w2c[:].rearrange("p (b t m) -> p b m t", b=2, t=4),
                        w2_raw[:].rearrange("p (b m t) -> p b m t", b=2, t=4))
-        vs3 = gather(ts3, o3, U8, "vs3", "vs3")
         vc2 = gather(tw2, o2, U32, "vc2", "vc2")
+        vs3 = gather(ts3, o3, U8, "vs3", "vs3")
         vs1 = gather(ts1, o1, U8, "vs1", "vs1")
-        g3 = cast_gpsimd(raw3)
-        raw1b = load_raw(w1[KP:2 * KP, :], "C")
-        p1 = load_list(pos1, "p1")
         tw0 = load_words(tab_words[0], "tw0", T, "T2")
-        course = keep.tile([P, 8, J], F32, name="course")
+        early = keep.tile([P, PACK, J], F32, name="early")
+        course = [early[:, r, :] for r in range(PACK)]
+        windows = []
         for r in range(8):
-            window = first_stage(r, [(w2c, w2s, vc2, vs2, 4)], "S%d" % r)
-            nc.vector.tensor_copy(course[:, r, :], window[:].indirect(p2[:]))
-            if r == 3:
+            windows.append(first_stage(r, [(w2c, w2s, vc2, vs2, 0)], "S%d" % r))
+            if r == PACK:
                 vc3 = gather(tw3, o3, U32, "vc3", "S3")
-                tw1 = load_words(tab_words[1], "tw1", T, "T3")
-            if r == 4:
-                w3c, w3s = quantize([g3], "w3", "S4")
+                middle = keep.tile([P, 2 + PACK, J], F32, name="middle", tag="T3", align_bytes=64)
+                course.extend([middle[:, 0, :], middle[:, 1, :]])
+            if r < EARLY:
+                nc.vector.tensor_copy(course[r], windows[r][:].indirect(p2[:]))
+        g3 = [cast_scalar(raw3, 0, "S2"), cast_scalar(raw3, 1, "S1")]
+        w3c, w3s = quantize(g3, "w3", "w3c")
+        tw1 = load_words(tab_words[1], "tw1", T, "A")
+        late = keep.tile([P, 8 - EARLY, J], F32, name="late", tag="S1", align_bytes=64)
+        for r in range(EARLY, 8):
+            course.append(late[:, r - EARLY, :])
+            nc.vector.tensor_copy(course[r], windows[r][:].indirect(p2[:]))
 
-        g1a = cast_gpsimd(raw1a)
         w4c = keep.tile([P, 2 * 2 * N], U8, name="w4c", align_bytes=64)
         nc.sync.dma_start(w4c[:].bitcast(I32).rearrange("p (a c) -> p a c", a=2),
                           w4_words.bitcast(I32).rearrange("a p c -> p a c"))
@@ -163,24 +171,23 @@ def tile_list_handicap_weight_book_kernel(
         with nc.allow_non_contiguous_dma(reason="one bias value a partition"):
             nc.sync.dma_start(bias_t[:], bias.rearrange("(c p) -> p c", p=P))
 
-        below = []
         for b in range(2):
             if b == 1:
+                g1a = [cast_scalar(raw1a, 0, "S5"), cast_scalar(raw1a, 1, "S0")]
+                g1b = [cast_scalar(raw1b, 0, "S13"), cast_scalar(raw1b, 1, "S2")]
                 vc0 = gather(tw0, o1, U32, "vc0", "S8")
-                g1b = cast_scalar(raw1b, ("S5", "S6"))
-                w1bc, w1bs = quantize(g1b, "w1b", "w1bc")
-                vc1 = gather(tw1, o1, U32, "vc1", "S6")
-                raw5 = keep.tile([P, 2, PACK, N], F32, name="raw", tag="C", align_bytes=64)
+                w1ac, w1as = quantize(g1a, "w1a", "T2")
+                vc1 = gather(tw1, o1, U32, "vc1", "vc1")
+                w1bc, w1bs = quantize(g1b, "w1b", "A")
+                raw5 = keep.tile([P, 2, PACK, N], F32, name="raw", tag="B", align_bytes=64)
                 for a in range(2):
                     nc.sync.dma_start(raw5[:, a], w5[KP * a:KP * (a + 1), :].rearrange("(p j) c -> p j c", j=PACK))
-            z = keep.tile([P, PACK, J], F32, name="z", tag=("A", "T3")[b], align_bytes=64)
-            below.append(z)
+                pairs = [keep.tile([P, 2, J], F32, name="pair", tag=tag, align_bytes=64) for tag in ("S13", "S2")]
             for t in range(PACK):
                 r = PACK * b + t
-                window = first_stage(r, [(w3c, w3s, vc3, vs3, 0)], D_TAGS[r])
-                nc.vector.tensor_tensor(z[:, t, :], window[:].indirect(p3[:]), course[:, r, :], ALU.subtract)
-                if r == 1:
-                    w1ac, w1as = quantize([g1a], "w1a", "S1")
+                window = first_stage(r, [(w3c, w3s, vc3, vs3, 4)], D_TAGS[r])
+                below = middle[:, 2 + t, :] if b == 0 else pairs[t // 2][:, t % 2, :]
+                nc.vector.tensor_tensor(below, window[:].indirect(p3[:]), course[r], ALU.subtract)
 
         a_passes = [(w1ac, w1as, vc0, vs1, 8), (w1bc, w1bs, vc1, vs1, 12)]
         zq = []
@@ -191,37 +198,34 @@ def tile_list_handicap_weight_book_kernel(
         def join(b, windows, c0, c1, lead):
             for t in range(PACK):
                 nc.vector.tensor_tensor(lead[:, t, :], windows[t][:].indirect(p1[:, c0 // 16:c1 // 16]),
-                                        course[:, PACK * b + t, c0:c1], ALU.subtract)
+                                        course[PACK * b + t][:, c0:c1], ALU.subtract)
             z = spread[b][:, :, c0:c1]
             nc.vector.scalar_tensor_tensor(z, lead[:], 0.0, z, ALU.max, ALU.add)
 
-        def round_z(b, c0, c1, tag):
+        def round_z(copy, b, c0, c1, tag):
             rounded = keep.tile([P, PACK * (c1 - c0)], BF16, name="rounded", tag=tag, align_bytes=64)
-            interleave(nc.scalar.copy, rounded[:], spread[b][:, :, c0:c1])
+            interleave(copy, rounded[:], spread[b][:, :, c0:c1])
             return rounded
 
         def quantize_z(b, c0, c1, rounded):
             nc.vector.quantize_mx(out=zq[b][0][:, c0:c1].bitcast(FP8X4), scales=zq[b][1][:, c0:c1], in_=rounded[:])
 
-        def lead_tile(pool, ci, tag):
-            c0, c1 = CHUNKS[ci]
-            return pool.tile([P, PACK, c1 - c0], F32, name="lead", tag=tag, align_bytes=64)
+        def lead_tile(width, tag):
+            return keep.tile([P, PACK, width], F32, name="lead", tag=tag, align_bytes=64)
 
-        def rectify(b, tag):
-            s = keep.tile([P, PACK, J], F32, name="spread", tag=tag, align_bytes=64)
-            nc.scalar.activation(s[:], below[b][:], ACT.Relu, scale=-1.0)
-            return s
-
-        spread = [rectify(0, "B")]
         windows0 = [first_stage(t, a_passes, A_TAGS[t]) for t in range(PACK)]
-        join(0, windows0, 0, J, keep.tile([P, PACK, J], F32, name="lead", tag="L", align_bytes=64))
+        spread = [middle[:, 2:, :]]
+        nc.scalar.activation(spread[0], spread[0], ACT.Relu, scale=-1.0)
+        join(0, windows0, 0, J, lead_tile(J, "L"))
         windows1 = [first_stage(PACK + t, a_passes, A_TAGS[PACK + t]) for t in range(PACK)]
-        rounded0 = round_z(0, 0, J, "zb0")
-        spread.append(rectify(1, "L"))
-        g5 = [keep.tile([P, PACK * N], BF16, name="g5", tag=tag, align_bytes=64) for tag in ("S11", "S7")]
-        for a in range(2):
-            interleave(nc.vector.tensor_copy, g5[a][:], raw5[:, a])
-        w5c, w5s = quantize(g5, "w5", "w5c")
+        second = keep.tile([P, PACK, J], F32, name="second", align_bytes=64)
+        spread.append(second[:])
+        for i in range(2):
+            nc.scalar.activation(second[:, 2 * i:2 * i + 2, :], pairs[i][:], ACT.Relu, scale=-1.0)
+        rounded0 = round_z(nc.scalar.copy, 0, 0, J, "zb0")
+        g5 = [keep.tile([P, PACK * N], BF16, name="g5", tag=tag, align_bytes=64) for tag in ("S5", "S7")]
+        interleave(nc.vector.tensor_copy, g5[0][:], raw5[:, 0])
+        interleave(nc.scalar.copy, g5[1][:], raw5[:, 1])
 
         tiles_n = N // P
         banks = []
@@ -229,7 +233,7 @@ def tile_list_handicap_weight_book_kernel(
             per_bank = BANK // (c1 - c0)
             banks.append([[psum.tile([P, BANK], F32, name="acc", tag="acc") for n0 in range(0, tiles_n, per_bank)]
                           for which in range(2)])
-        tail = keep.tile([P, 2, tiles_n * J], F32, name="tail", tag="T2", align_bytes=64)
+        bent = keep.tile([P, tiles_n * J], F32, name="bent", tag="bent", align_bytes=64)
 
         def second_stage(ci, which, b):
             c0, c1 = CHUNKS[ci]
@@ -247,36 +251,47 @@ def tile_list_handicap_weight_book_kernel(
                                     rhs=zq[b][0][:, c0:c1].bitcast(FP8X4), rhs_scale=zq[b][1][:, c0:c1],
                                     start=(b == 0 and slot == 0), stop=(b == 1 and slot == per_bank - 1))
 
-        def finish(ci):
+        def bend(ci):
             c0, c1 = CHUNKS[ci]
             width = c1 - c0
             per_bank = BANK // width
             base = tiles_n * c0
             for n in range(tiles_n):
                 slot = n % per_bank
-                nc.scalar.activation(tail[:, 0, base + width * n:base + width * (n + 1)],
+                nc.scalar.activation(bent[:, base + width * n:base + width * (n + 1)],
                                      banks[ci][0][n // per_bank][:, width * slot:width * (slot + 1)],
                                      ACT.Silu, bias=bias_t[:, n:n + 1])
+
+        def finish(ci, result):
+            c0, c1 = CHUNKS[ci]
+            width = c1 - c0
+            per_bank = BANK // width
+            base = tiles_n * c0
             for i, bank in enumerate(banks[ci][1]):
                 cols = slice(base + BANK * i, base + BANK * (i + 1))
-                nc.vector.tensor_tensor(tail[:, 1, cols], bank[:], tail[:, 0, cols], ALU.add)
+                nc.vector.tensor_tensor(result[:, cols], bank[:], bent[:, cols], ALU.add)
                 nc.sync.dma_start(
                     out.rearrange("(n p) j -> p n j", p=P)[:, per_bank * i:per_bank * (i + 1), c0:c1],
-                    tail[:, 1, cols].rearrange("p (n j) -> p n j", j=width))
+                    result[:, cols].rearrange("p (n j) -> p n j", j=width))
 
-        join(1, windows1, *CHUNKS[0], lead_tile(keep, 0, "C"))
-        rounded = round_z(1, *CHUNKS[0], "zb1")
+        join(1, windows1, *JOINS[0], lead_tile(JOINS[0][1], "L"))
+        rounded1 = round_z(nc.scalar.copy, 1, *JOINS[0], "zb1")
         quantize_z(0, 0, J, rounded0)
+        w5c, w5s = quantize(g5, "w5", "w5c")
         for which in range(2):
             for ci in range(len(CHUNKS)):
                 second_stage(ci, which, 0)
-        join(1, windows1, *CHUNKS[1], lead_tile(keep, 1, "zb0"))
-        for ci in range(len(CHUNKS)):
-            quantize_z(1, *CHUNKS[ci], rounded)
+        quantize_z(1, *JOINS[0], rounded1)
+        join(1, windows1, *JOINS[1], lead_tile(JOINS[1][1] - JOINS[1][0], "zb1"))
+        rounded2 = round_z(nc.vector.tensor_copy, 1, *JOINS[1], "zb2")
+        for ci in range(2):
             second_stage(ci, 0, 1)
             second_stage(ci, 1, 1)
-            if ci + 1 < len(CHUNKS):
-                rounded = round_z(1, *CHUNKS[ci + 1], "zb%d" % (ci + 2))
-            if ci + 2 < len(CHUNKS):
-                join(1, windows1, *CHUNKS[ci + 2], lead_tile(keep, ci + 2, "zb1"))
-            finish(ci)
+            bend(ci)
+        quantize_z(1, *JOINS[1], rounded2)
+        second_stage(2, 0, 1)
+        second_stage(2, 1, 1)
+        bend(2)
+        result = keep.tile([P, tiles_n * J], F32, name="result", tag="zb1", align_bytes=64)
+        for ci in range(len(CHUNKS)):
+            finish(ci, result)

@@ -78,17 +78,17 @@ def tile_list_handicap_weight_book_kernel(
 
         def quantize(pieces, name, tag):
             codes = keep.tile([P, H], U32, name=name + "_codes", tag=tag, align_bytes=64)
-            scales = keep.tile([P, H], U8, name=name + "_scales", align_bytes=64)
+            scales = keep.tile([P, H], U8, name=name + "_scales", tag=name + "_scales", align_bytes=64)
             width = H // len(pieces)
             for i, grouped in enumerate(pieces):
                 cols = slice(width * i, width * (i + 1))
                 nc.vector.quantize_mx(out=codes[:, cols].bitcast(FP8X4), scales=scales[:, cols], in_=grouped[:])
             return codes, scales
 
-        def cast_scalar(raw, b, tag):
+        def cast(copy, raw, b, tag):
             src = raw[:].rearrange("p (u e) (b m t) -> p b m u t e", u=2, b=2, t=4)
             grouped = keep.tile([P, PACK * KP], BF16, name="grouped", tag=tag, align_bytes=64)
-            nc.scalar.copy(grouped[:].rearrange("p (t m u e) -> p m u t e", t=4, u=2, e=2), src[:, b])
+            copy(grouped[:].rearrange("p (t m u e) -> p m u t e", t=4, u=2, e=2), src[:, b])
             return grouped
 
         def interleave(copy, dst, src):
@@ -112,7 +112,6 @@ def tile_list_handicap_weight_book_kernel(
 
         ts3 = zeroed_plane(T, "ts3")
         ts1 = zeroed_plane(T, "ts1")
-        w4s = zeroed_plane(2 * N, "w4s")
         o2 = load_list(offs2, "o2")
         ts2 = filled_plane(tab2_scales, "ts2")
         w2s_raw = filled_plane(w2_scales, "w2s_raw")
@@ -153,7 +152,7 @@ def tile_list_handicap_weight_book_kernel(
                 course.extend([middle[:, 0, :], middle[:, 1, :]])
             if r < EARLY:
                 nc.vector.tensor_copy(course[r], windows[r][:].indirect(p2[:]))
-        g3 = [cast_scalar(raw3, 0, "S2"), cast_scalar(raw3, 1, "S1")]
+        g3 = [cast(nc.scalar.copy, raw3, 0, "S2"), cast(nc.scalar.copy, raw3, 1, "S1")]
         w3c, w3s = quantize(g3, "w3", "w3c")
         tw1 = load_words(tab_words[1], "tw1", T, "A")
         late = keep.tile([P, 8 - EARLY, J], F32, name="late", tag="S1", align_bytes=64)
@@ -161,20 +160,11 @@ def tile_list_handicap_weight_book_kernel(
             course.append(late[:, r - EARLY, :])
             nc.vector.tensor_copy(course[r], windows[r][:].indirect(p2[:]))
 
-        w4c = keep.tile([P, 2 * 2 * N], U8, name="w4c", align_bytes=64)
-        nc.sync.dma_start(w4c[:].bitcast(I32).rearrange("p (a c) -> p a c", a=2),
-                          w4_words.bitcast(I32).rearrange("a p c -> p a c"))
-        for q in range(4):
-            nc.sync.dma_start(w4s[32 * q:32 * q + 4, :].bitcast(I32).rearrange("p (a c) -> p a c", a=2),
-                              w4_scales[:, 4 * q:4 * q + 4, :].bitcast(I32).rearrange("a r c -> r a c"))
-        bias_t = keep.tile([P, N // P], F32, name="bias_t")
-        with nc.allow_non_contiguous_dma(reason="one bias value a partition"):
-            nc.sync.dma_start(bias_t[:], bias.rearrange("(c p) -> p c", p=P))
 
         for b in range(2):
             if b == 1:
-                g1a = [cast_scalar(raw1a, 0, "S5"), cast_scalar(raw1a, 1, "S0")]
-                g1b = [cast_scalar(raw1b, 0, "S13"), cast_scalar(raw1b, 1, "S2")]
+                g1a = [cast(nc.scalar.copy, raw1a, 0, "S5"), cast(nc.scalar.copy, raw1a, 1, "S0")]
+                g1b = [cast(nc.scalar.copy, raw1b, 0, "S13"), cast(nc.vector.tensor_copy, raw1b, 1, "S2")]
                 vc0 = gather(tw0, o1, U32, "vc0", "S8")
                 w1ac, w1as = quantize(g1a, "w1a", "T2")
                 vc1 = gather(tw1, o1, U32, "vc1", "vc1")
@@ -188,6 +178,18 @@ def tile_list_handicap_weight_book_kernel(
                 window = first_stage(r, [(w3c, w3s, vc3, vs3, 4)], D_TAGS[r])
                 below = middle[:, 2 + t, :] if b == 0 else pairs[t // 2][:, t % 2, :]
                 nc.vector.tensor_tensor(below, window[:].indirect(p3[:]), course[r], ALU.subtract)
+
+        w4c = keep.tile([P, 2 * 2 * N], U8, name="w4c", tag="w3c", align_bytes=64)
+        nc.sync.dma_start(w4c[:].bitcast(I32).rearrange("p (a c) -> p a c", a=2),
+                          w4_words.bitcast(I32).rearrange("a p c -> p a c"))
+        w4s = keep.tile([P, 2 * N], U8, name="w4s", tag="w3_scales", align_bytes=64)
+        nc.gpsimd.memset(w4s[:].bitcast(I32), 0)
+        for q in range(4):
+            nc.sync.dma_start(w4s[32 * q:32 * q + 4, :].bitcast(I32).rearrange("p (a c) -> p a c", a=2),
+                              w4_scales[:, 4 * q:4 * q + 4, :].bitcast(I32).rearrange("a r c -> r a c"))
+        bias_t = keep.tile([P, N // P], F32, name="bias_t", tag="vs3", align_bytes=64)
+        with nc.allow_non_contiguous_dma(reason="one bias value a partition"):
+            nc.sync.dma_start(bias_t[:], bias.rearrange("(c p) -> p c", p=P))
 
         a_passes = [(w1ac, w1as, vc0, vs1, 8), (w1bc, w1bs, vc1, vs1, 12)]
         zq = []

@@ -47,19 +47,14 @@ def tile_list_handicap_weight_book_kernel(
             nc.vector.memset(t[:].bitcast(I32), 0)
             return t
 
-        def load_plane(queue, t, scales, first):
-            passes = scales.shape[0]
-            for q in range(4):
-                lo = 32 * q + first
-                queue.dma_start(t[lo:lo + 4 * passes, :].bitcast(I32), scales[:, 4 * q:4 * q + 4, :].bitcast(I32))
-
-        def filled_plane(scales, name):
-            width = scales.shape[2]
-            t = keep.tile([P, width], U8, name=name, align_bytes=64)
-            for q in range(4):
-                live = scales[:, 4 * q:4 * q + 4, :].bitcast(I32)
-                nc.sync.dma_start(t[32 * q:32 * (q + 1), :].bitcast(I32), live.broadcast_to([8, 4, width // 4]))
-            return t
+        def load_plane(t, scales, first):
+            if scales.shape[0] == 1:
+                for r in range(4):
+                    nc.sync.dma_start(t[first + r:P:32, :].bitcast(I32), scales[0, r:16:4, :].bitcast(I32))
+            else:
+                for q in range(4):
+                    lo = 32 * q + first
+                    nc.sync.dma_start(t[lo:lo + 8, :].bitcast(I32), scales[:, 4 * q:4 * q + 4, :].bitcast(I32))
 
         def load_words(words, name, width, tag):
             t = keep.tile([P, width], U32, name=name, tag=tag, align_bytes=64)
@@ -110,19 +105,21 @@ def tile_list_handicap_weight_book_kernel(
                 nc.scalar.copy(window[:, half], acc[:])
             return window
 
+        ts2 = zeroed_plane(T, "ts2")
+        w2s_raw = zeroed_plane(H, "w2s_raw")
         ts3 = zeroed_plane(T, "ts3")
         ts1 = zeroed_plane(T, "ts1")
         o2 = load_list(offs2, "o2")
-        ts2 = filled_plane(tab2_scales, "ts2")
-        w2s_raw = filled_plane(w2_scales, "w2s_raw")
         tw2 = load_words(tab2_words[0], "tw2", T, "T2")
         w2_raw = load_words(w2_words[0], "w2_raw", H, "w2_raw")
+        load_plane(ts2, tab2_scales, 0)
+        load_plane(w2s_raw, w2_scales, 0)
         o3 = load_list(offs3, "o3")
-        load_plane(nc.sync, ts3, tab3_scales, 4)
+        load_plane(ts3, tab3_scales, 4)
         o1 = load_list(offs, "o1")
-        load_plane(nc.sync, ts1, tab_scales, 8)
-        raw3 = load_raw(w3, "A")
+        load_plane(ts1, tab_scales, 8)
         p2 = load_list(pos2, "p2")
+        raw3 = load_raw(w3, "A")
         tw3 = load_words(tab3_words[0], "tw3", T, "T3")
         p3 = load_list(pos3, "p3")
         raw1a = load_raw(w1[0:KP, :], "B")
@@ -130,6 +127,7 @@ def tile_list_handicap_weight_book_kernel(
         nc.sync.dma_start(raw1b[:], w1[KP:2 * KP, :].rearrange("(p j) c -> p j c", j=PACK))
         p1 = load_list(pos1, "p1")
 
+        vc2 = gather(tw2, o2, U32, "vc2", "vc2")
         vs2 = gather(ts2, o2, U8, "vs2", "vs2")
         w2s = keep.tile([P, H], U8, name="w2s", align_bytes=64)
         nc.vector.tensor_copy(w2s[:].rearrange("p (b t m) -> p b t m", b=2, t=4),
@@ -137,7 +135,6 @@ def tile_list_handicap_weight_book_kernel(
         w2c = keep.tile([P, H], U32, name="w2c", align_bytes=64)
         nc.scalar.copy(w2c[:].rearrange("p (b t m) -> p b m t", b=2, t=4),
                        w2_raw[:].rearrange("p (b m t) -> p b m t", b=2, t=4))
-        vc2 = gather(tw2, o2, U32, "vc2", "vc2")
         vs3 = gather(ts3, o3, U8, "vs3", "vs3")
         vs1 = gather(ts1, o1, U8, "vs1", "vs1")
         tw0 = load_words(tab_words[0], "tw0", T, "T2")
@@ -184,9 +181,9 @@ def tile_list_handicap_weight_book_kernel(
                           w4_words.bitcast(I32).rearrange("a p c -> p a c"))
         w4s = keep.tile([P, 2 * N], U8, name="w4s", tag="w3_scales", align_bytes=64)
         nc.gpsimd.memset(w4s[:].bitcast(I32), 0)
-        for q in range(4):
-            nc.sync.dma_start(w4s[32 * q:32 * q + 4, :].bitcast(I32).rearrange("p (a c) -> p a c", a=2),
-                              w4_scales[:, 4 * q:4 * q + 4, :].bitcast(I32).rearrange("a r c -> r a c"))
+        for r in range(4):
+            nc.sync.dma_start(w4s[r:P:32, :].bitcast(I32).rearrange("p (a c) -> p a c", a=2),
+                              w4_scales[:, r:16:4, :].bitcast(I32).rearrange("a q c -> q a c"))
         bias_t = keep.tile([P, N // P], F32, name="bias_t", tag="vs3", align_bytes=64)
         with nc.allow_non_contiguous_dma(reason="one bias value a partition"):
             nc.sync.dma_start(bias_t[:], bias.rearrange("(c p) -> p c", p=P))

from contextlib import ExitStack

import concourse.mybir as mybir

F32 = mybir.dt.float32
BF16 = mybir.dt.bfloat16
I32 = mybir.dt.int32
U32 = mybir.dt.uint32
U16 = mybir.dt.uint16
U8 = mybir.dt.uint8
FP8X4 = mybir.dt.float8_e4m3fn_x4
FP4X4 = mybir.dt.float4_e2m1fn_x4
ALU = mybir.AluOpType
ACT = mybir.ActivationFunctionType

K, K2, H, N, T, S, J = 1024, 512, 1024, 512, 4096, 1024, 512
P = 128
PACK = 4
KP = P * PACK
BANK = 512
CHUNKS = ((0, 256), (256, 384), (384, 512))
JOINS = ((0, 384), (384, 512))
EARLY = 6
D_TAGS = ("S0", "S13", "S2", "S8", 0, 1, 2, 3)
A_TAGS = ("S6", "S7", "S4", "S5", "S3", "S0", 0, 1)
FLOPS = 2 * (K + 2 * K2) * H * S + 2 * 2 * H * N * J


def tile_list_handicap_weight_book_kernel(
    tc, tab_words, tab_scales, tab2_words, tab2_scales, tab3_words, tab3_scales, offs, offs2, offs3,
    pos1, pos2, pos3, w1, w2_words, w2_scales, w3, w4_words, w4_scales, bias, w5, out,
):
    nc = tc.nc
    with ExitStack() as ctx:
        lists = ctx.enter_context(tc.tile_pool(name="lists", bufs=1))
        keep = ctx.enter_context(tc.tile_pool(name="keep", bufs=1))
        placed = ctx.enter_context(tc.tile_pool(name="placed", bufs=1))
        psum = ctx.enter_context(tc.psum_pool(name="psum", bufs=8))

        def load_list(src, name):
            t = lists.tile(list(src.shape), U16, name=name)
            nc.sync.dma_start(t[:], src)
            return t

        def zeroed_plane(width, name):
            t = keep.tile([P, width], U8, name=name, align_bytes=64)
            nc.vector.memset(t[:].bitcast(I32), 0)
            return t

        def load_plane(t, scales, first):
            if scales.shape[0] == 1:
                for r in range(4):
                    nc.sync.dma_start(t[first + r:P:32, :].bitcast(I32), scales[0, r:16:4, :].bitcast(I32))
            else:
                for q in range(4):
                    lo = 32 * q + first
                    nc.sync.dma_start(t[lo:lo + 8, :].bitcast(I32), scales[:, 4 * q:4 * q + 4, :].bitcast(I32))

        def load_words(words, name, width, tag):
            t = keep.tile([P, width], U32, name=name, tag=tag, align_bytes=64)
            nc.sync.dma_start(t[:].bitcast(I32), words.rearrange("p t i -> p (t i)").bitcast(I32))
            return t

        def load_raw(src, tag):
            t = keep.tile([P, PACK, H], F32, name="raw", tag=tag, align_bytes=64)
            nc.sync.dma_start(t[:], src.rearrange("(p j) c -> p j c", j=PACK))
            return t

        def gather(window, offsets, dtype, name, tag):
            t = keep.tile([P, S], dtype, name=name, tag=tag, align_bytes=64)
            nc.vector.tensor_copy(t[:], window[:].indirect(offsets[:]))
            return t

        def quantize(pieces, name, tag):
            codes = keep.tile([P, H], U32, name=name + "_codes", tag=tag, align_bytes=64)
            scales = keep.tile([P, H], U8, name=name + "_scales", tag=name + "_scales", align_bytes=64)
            width = H // len(pieces)
            for i, grouped in enumerate(pieces):
                cols = slice(width * i, width * (i + 1))
                nc.vector.quantize_mx(out=codes[:, cols].bitcast(FP8X4), scales=scales[:, cols], in_=grouped[:])
            return codes, scales

        def cast(copy, raw, b, tag):
            src = raw[:].rearrange("p (u e) (b m t) -> p b m u t e", u=2, b=2, t=4)
            grouped = keep.tile([P, PACK * KP], BF16, name="grouped", tag=tag, align_bytes=64)
            copy(grouped[:].rearrange("p (t m u e) -> p m u t e", t=4, u=2, e=2), src[:, b])
            return grouped

        def interleave(copy, dst, src):
            copy(dst.rearrange("p (c i j) -> p c j i", i=4, j=PACK), src.rearrange("p j (c i) -> p c j i", i=4))

        def first_stage(r, passes, tag):
            if isinstance(tag, int):
                window = placed.tile([P, S], F32, name="window%d_%d" % (len(passes), r), offset=4 * S * tag, align_bytes=64)
            else:
                window = keep.tile([P, S], F32, name="window", tag=tag, align_bytes=64)
            cols = slice(P * r, P * (r + 1))
            for h in range(S // BANK):
                acc = psum.tile([P, BANK], F32, name="acc", tag="acc")
                half = slice(BANK * h, BANK * (h + 1))
                for a, (wc, ws, vc, vs, first) in enumerate(passes):
                    nc.tensor.matmul_mx(out=acc[:], lhsT=wc[:, cols].bitcast(FP8X4), lhsT_scale=ws[:, cols],
                                        rhs=vc[:, half].bitcast(FP8X4), rhs_scale=vs[first:, half],
                                        start=(a == 0), stop=(a == len(passes) - 1))
                nc.scalar.copy(window[:, half], acc[:])
            return window

        ts2 = zeroed_plane(T, "ts2")
        w2s_raw = zeroed_plane(H, "w2s_raw")
        ts3 = zeroed_plane(T, "ts3")
        ts1 = zeroed_plane(T, "ts1")
        o2 = load_list(offs2, "o2")
        tw2 = load_words(tab2_words[0], "tw2", T, "T2")
        w2_raw = load_words(w2_words[0], "w2_raw", H, "w2_raw")
        load_plane(ts2, tab2_scales, 0)
        load_plane(w2s_raw, w2_scales, 0)
        o3 = load_list(offs3, "o3")
        load_plane(ts3, tab3_scales, 4)
        o1 = load_list(offs, "o1")
        load_plane(ts1, tab_scales, 8)
        p2 = load_list(pos2, "p2")
        raw3 = load_raw(w3, "A")
        tw3 = load_words(tab3_words[0], "tw3", T, "T3")
        p3 = load_list(pos3, "p3")
        raw1a = load_raw(w1[0:KP, :], "B")
        raw1b = placed.tile([P, PACK, H], F32, name="raw1b", offset=0, align_bytes=64)
        nc.sync.dma_start(raw1b[:], w1[KP:2 * KP, :].rearrange("(p j) c -> p j c", j=PACK))
        p1 = load_list(pos1, "p1")

        vc2 = gather(tw2, o2, U32, "vc2", "vc2")
        vs2 = gather(ts2, o2, U8, "vs2", "vs2")
        w2s = keep.tile([P, H], U8, name="w2s", align_bytes=64)
        nc.vector.tensor_copy(w2s[:].rearrange("p (b t m) -> p b t m", b=2, t=4),
                              w2s_raw[:].rearrange("p (b m t) -> p b t m", b=2, t=4))
        w2c = keep.tile([P, H], U32, name="w2c", align_bytes=64)
        nc.scalar.copy(w2c[:].rearrange("p (b t m) -> p b m t", b=2, t=4),
                       w2_raw[:].rearrange("p (b m t) -> p b m t", b=2, t=4))
        vs3 = gather(ts3, o3, U8, "vs3", "vs3")
        vs1 = gather(ts1, o1, U8, "vs1", "vs1")
        tw0 = load_words(tab_words[0], "tw0", T, "T2")
        early = keep.tile([P, PACK, J], F32, name="early")
        course = [early[:, r, :] for r in range(PACK)]
        windows = []
        for r in range(8):
            windows.append(first_stage(r, [(w2c, w2s, vc2, vs2, 0)], "S%d" % r))
            if r == PACK:
                vc3 = gather(tw3, o3, U32, "vc3", "S3")
                middle = keep.tile([P, 2 + PACK, J], F32, name="middle", tag="T3", align_bytes=64)
                course.extend([middle[:, 0, :], middle[:, 1, :]])
            if r < EARLY:
                nc.vector.tensor_copy(course[r], windows[r][:].indirect(p2[:]))
        g3 = [cast(nc.scalar.copy, raw3, 0, "S2"), cast(nc.scalar.copy, raw3, 1, "S1")]
        w3c, w3s = quantize(g3, "w3", "w3c")
        tw1 = load_words(tab_words[1], "tw1", T, "A")
        late = keep.tile([P, 8 - EARLY, J], F32, name="late", tag="S1", align_bytes=64)
        for r in range(EARLY, 8):
            course.append(late[:, r - EARLY, :])
            nc.vector.tensor_copy(course[r], windows[r][:].indirect(p2[:]))


        for b in range(2):
            if b == 1:
                g1a = [cast(nc.scalar.copy, raw1a, 0, "S5"), cast(nc.scalar.copy, raw1a, 1, "S0")]
                g1b = [cast(nc.scalar.copy, raw1b, 0, "S13"), cast(nc.vector.tensor_copy, raw1b, 1, "S2")]
                vc0 = gather(tw0, o1, U32, "vc0", "S8")
                w1ac, w1as = quantize(g1a, "w1a", "T2")
                vc1 = gather(tw1, o1, U32, "vc1", "vc1")
                w1bc, w1bs = quantize(g1b, "w1b", "A")
                raw5 = keep.tile([P, 2, PACK, N], F32, name="raw", tag="B", align_bytes=64)
                for a in range(2):
                    nc.sync.dma_start(raw5[:, a], w5[KP * a:KP * (a + 1), :].rearrange("(p j) c -> p j c", j=PACK))
                pairs = [keep.tile([P, 2, J], F32, name="pair", tag=tag, align_bytes=64) for tag in ("S13", "S2")]
            for t in range(PACK):
                r = PACK * b + t
                window = first_stage(r, [(w3c, w3s, vc3, vs3, 4)], D_TAGS[r])
                below = middle[:, 2 + t, :] if b == 0 else pairs[t // 2][:, t % 2, :]
                nc.vector.tensor_tensor(below, window[:].indirect(p3[:]), course[r], ALU.subtract)

        w4c = keep.tile([P, 2 * 2 * N], U8, name="w4c", tag="w3c", align_bytes=64)
        nc.sync.dma_start(w4c[:].bitcast(I32).rearrange("p (a c) -> p a c", a=2),
                          w4_words.bitcast(I32).rearrange("a p c -> p a c"))
        w4s = keep.tile([P, 2 * N], U8, name="w4s", tag="w3_scales", align_bytes=64)
        nc.gpsimd.memset(w4s[:].bitcast(I32), 0)
        for r in range(4):
            nc.sync.dma_start(w4s[r:P:32, :].bitcast(I32).rearrange("p (a c) -> p a c", a=2),
                              w4_scales[:, r:16:4, :].bitcast(I32).rearrange("a q c -> q a c"))
        bias_t = keep.tile([P, N // P], F32, name="bias_t", tag="vs3", align_bytes=64)
        with nc.allow_non_contiguous_dma(reason="one bias value a partition"):
            nc.sync.dma_start(bias_t[:], bias.rearrange("(c p) -> p c", p=P))

        a_passes = [(w1ac, w1as, vc0, vs1, 8), (w1bc, w1bs, vc1, vs1, 12)]
        zq = []
        for b in range(2):
            zq.append((keep.tile([P, J], U32, name="z_codes%d" % b, align_bytes=64),
                       keep.tile([P, J], U8, name="z_scales%d" % b, align_bytes=64)))

        def join(b, windows, c0, c1, lead):
            for t in range(PACK):
                nc.vector.tensor_tensor(lead[:, t, :], windows[t][:].indirect(p1[:, c0 // 16:c1 // 16]),
                                        course[PACK * b + t][:, c0:c1], ALU.subtract)
            z = spread[b][:, :, c0:c1]
            nc.vector.scalar_tensor_tensor(z, lead[:], 0.0, z, ALU.max, ALU.add)

        def round_z(copy, b, c0, c1, tag):
            rounded = keep.tile([P, PACK * (c1 - c0)], BF16, name="rounded", tag=tag, align_bytes=64)
            interleave(copy, rounded[:], spread[b][:, :, c0:c1])
            return rounded

        def quantize_z(b, c0, c1, rounded):
            nc.vector.quantize_mx(out=zq[b][0][:, c0:c1].bitcast(FP8X4), scales=zq[b][1][:, c0:c1], in_=rounded[:])

        def lead_tile(width, tag):
            return keep.tile([P, PACK, width], F32, name="lead", tag=tag, align_bytes=64)

        windows0 = [first_stage(t, a_passes, A_TAGS[t]) for t in range(PACK)]
        spread = [middle[:, 2:, :]]
        nc.scalar.activation(spread[0], spread[0], ACT.Relu, scale=-1.0)
        join(0, windows0, 0, J, lead_tile(J, "L"))
        windows1 = [first_stage(PACK + t, a_passes, A_TAGS[PACK + t]) for t in range(PACK)]
        second = keep.tile([P, PACK, J], F32, name="second", align_bytes=64)
        spread.append(second[:])
        for i in range(2):
            nc.scalar.activation(second[:, 2 * i:2 * i + 2, :], pairs[i][:], ACT.Relu, scale=-1.0)
        rounded0 = round_z(nc.scalar.copy, 0, 0, J, "zb0")
        g5 = [keep.tile([P, PACK * N], BF16, name="g5", tag=tag, align_bytes=64) for tag in ("S5", "S7")]
        interleave(nc.vector.tensor_copy, g5[0][:], raw5[:, 0])
        interleave(nc.scalar.copy, g5[1][:], raw5[:, 1])

        tiles_n = N // P
        banks = []
        for c0, c1 in CHUNKS:
            per_bank = BANK // (c1 - c0)
            banks.append([[psum.tile([P, BANK], F32, name="acc", tag="acc") for n0 in range(0, tiles_n, per_bank)]
                          for which in range(2)])
        bent = keep.tile([P, tiles_n * J], F32, name="bent", tag="bent", align_bytes=64)

        def second_stage(ci, which, b):
            c0, c1 = CHUNKS[ci]
            width = c1 - c0
            per_bank = BANK // width
            for n in range(tiles_n):
                col = N * b + P * n
                if which == 0:
                    lhsT, lhsT_scale = w4c[:, 2 * col:2 * (col + P)].bitcast(FP4X4), w4s[:, col:col + P]
                else:
                    lhsT, lhsT_scale = w5c[:, col:col + P].bitcast(FP8X4), w5s[:, col:col + P]
                slot = n % per_bank
                nc.tensor.matmul_mx(out=banks[ci][which][n // per_bank][:, width * slot:width * (slot + 1)],
                                    lhsT=lhsT, lhsT_scale=lhsT_scale,
                                    rhs=zq[b][0][:, c0:c1].bitcast(FP8X4), rhs_scale=zq[b][1][:, c0:c1],
                                    start=(b == 0 and slot == 0), stop=(b == 1 and slot == per_bank - 1))

        def bend(ci):
            c0, c1 = CHUNKS[ci]
            width = c1 - c0
            per_bank = BANK // width
            base = tiles_n * c0
            for n in range(tiles_n):
                slot = n % per_bank
                nc.scalar.activation(bent[:, base + width * n:base + width * (n + 1)],
                                     banks[ci][0][n // per_bank][:, width * slot:width * (slot + 1)],
                                     ACT.Silu, bias=bias_t[:, n:n + 1])

        def finish(ci, result):
            c0, c1 = CHUNKS[ci]
            width = c1 - c0
            per_bank = BANK // width
            base = tiles_n * c0
            for i, bank in enumerate(banks[ci][1]):
                cols = slice(base + BANK * i, base + BANK * (i + 1))
                nc.vector.tensor_tensor(result[:, cols], bank[:], bent[:, cols], ALU.add)
                nc.sync.dma_start(
                    out.rearrange("(n p) j -> p n j", p=P)[:, per_bank * i:per_bank * (i + 1), c0:c1],
                    result[:, cols].rearrange("p (n j) -> p n j", j=width))

        join(1, windows1, *JOINS[0], lead_tile(JOINS[0][1], "L"))
        rounded1 = round_z(nc.scalar.copy, 1, *JOINS[0], "zb1")
        quantize_z(0, 0, J, rounded0)
        w5c, w5s = quantize(g5, "w5", "w5c")
        for which in range(2):
            for ci in range(len(CHUNKS)):
                second_stage(ci, which, 0)
        quantize_z(1, *JOINS[0], rounded1)
        join(1, windows1, *JOINS[1], lead_tile(JOINS[1][1] - JOINS[1][0], "zb1"))
        rounded2 = round_z(nc.vector.tensor_copy, 1, *JOINS[1], "zb2")
        for ci in range(2):
            second_stage(ci, 0, 1)
            second_stage(ci, 1, 1)
            bend(ci)
        quantize_z(1, *JOINS[1], rounded2)
        second_stage(2, 0, 1)
        second_stage(2, 1, 1)
        bend(2)
        result = keep.tile([P, tiles_n * J], F32, name="result", tag="zb1", align_bytes=64)
        for ci in range(len(CHUNKS)):
            finish(ci, result)
